import numpy as np
import ml_dtypes

BF16 = ml_dtypes.bfloat16


def bf(x):
    return np.asarray(x, np.float32).astype(BF16)


def f32(x):
    return np.asarray(x, np.float32)


def f64(x):
    return np.asarray(x).astype(np.float64)


def striped(idx):
    return np.tile(idx.reshape(-1, 16).T, (8, 1))


def rows(idx, k):
    return np.tile(idx, (k, 1))


def look(tab, idx):
    return np.take_along_axis(f64(tab), rows(idx, len(tab)), axis=1)


K, S, V, N, M = 128, 256, 64, 64, 128


def setup_inputs():
    return {"tab": f32(np.random.standard_normal((K, S))), "y": f32(np.random.standard_normal((K, V))), "w": bf(np.random.standard_normal((K, M)) / np.sqrt(K)), "offs": striped(np.random.permutation(S)[:N])}


def reference(tab, y, w, offs):
    idx = offs[:16].T.reshape(-1)
    t = look(tab, idx)
    x = np.maximum(t, 0.0) * f64(y)
    y = f64(w).T @ x
    return y

@@ -1,0 +1,40 @@
+import concourse.mybir as mybir
+
+BF16, F32, U16 = mybir.dt.bfloat16, mybir.dt.float32, mybir.dt.uint16
+RELU = mybir.ActivationFunctionType.Relu
+MULT = mybir.AluOpType.mult
+
+R, S, N, M = 128, 256, 64, 128
+OFFSETS_IN_A_COLUMN = 16
+
+FLOPS = 2 * R * M * N + 2 * R * N
+BYTES = R * S * 4 + R * N * 4 + R * M * 2 + R * (N // OFFSETS_IN_A_COLUMN) * 2 + M * N * 4
+
+
+def tile_lookup_gate_relu_none_kernel(tc, tab, y, w, offs, out):
+    nc = tc.nc
+    with (
+        tc.tile_pool(name="held", bufs=1) as held,
+        tc.psum_pool(name="psum", bufs=1) as psum,
+    ):
+        offsets = held.tile([R, N // OFFSETS_IN_A_COLUMN], U16)
+        table = held.tile([R, S], F32)
+        stream = held.tile([R, N], F32)
+        weights = held.tile([R, M], BF16)
+        nc.sync.dma_start(offsets[:], offs)
+        nc.sync.dma_start(table[:], tab)
+        nc.scalar.dma_start(stream[:], y)
+        nc.scalar.dma_start(weights[:], w)
+
+        gate = held.tile([R, N], F32)
+        nc.scalar.activation(gate[:], table[:].indirect(offsets[:]), RELU)
+
+        x = held.tile([R, N], BF16)
+        nc.vector.tensor_tensor(x[:], gate[:], stream[:], MULT)
+
+        product = psum.tile([M, N], F32)
+        nc.tensor.matmul(product[:], weights[:], x[:], start=True, stop=True)
+
+        result = held.tile([M, N], F32)
+        nc.vector.tensor_copy(result[:], product[:])
+        nc.sync.dma_start(out, result[:])

@@ -26,6 +26,11 @@ def tile_lookup_gate_relu_none_kernel(tc, tab, y, w, offs, out):
         nc.scalar.dma_start(stream[:], y)
         nc.scalar.dma_start(weights[:], w)
 
+        zeros = held.tile([R, 1], F32)
+        nc.vector.memset(zeros[:], 0.0)
+        warm = held.tile([R, 1], F32)
+        nc.scalar.activation(warm[:], zeros[:], RELU)
+
         gate = held.tile([R, N], F32)
         nc.scalar.activation(gate[:], table[:].indirect(offsets[:]), RELU)
 

@@ -22,9 +22,9 @@ def tile_lookup_gate_relu_none_kernel(tc, tab, y, w, offs, out):
         stream = held.tile([R, N], F32)
         weights = held.tile([R, M], BF16)
         nc.sync.dma_start(offsets[:], offs)
-        nc.sync.dma_start(table[:], tab)
-        nc.scalar.dma_start(stream[:], y)
-        nc.scalar.dma_start(weights[:], w)
+        nc.scalar.dma_start(table[:], tab)
+        nc.sync.dma_start(stream[:], y)
+        nc.sync.dma_start(weights[:], w)
 
         zeros = held.tile([R, 1], F32)
         nc.vector.memset(zeros[:], 0.0)

@@ -41,5 +41,5 @@ def tile_lookup_gate_relu_none_kernel(tc, tab, y, w, offs, out):
         nc.tensor.matmul(product[:], weights[:], x[:], start=True, stop=True)
 
         result = held.tile([M, N], F32)
-        nc.vector.tensor_copy(result[:], product[:])
-        nc.sync.dma_start(out, result[:])
+        nc.scalar.copy(result[:], product[:])
+        nc.scalar.dma_start(out, result[:])

import concourse.mybir as mybir

BF16, F32, U16 = mybir.dt.bfloat16, mybir.dt.float32, mybir.dt.uint16
RELU = mybir.ActivationFunctionType.Relu
MULT = mybir.AluOpType.mult

R, S, N, M = 128, 256, 64, 128
OFFSETS_IN_A_COLUMN = 16

FLOPS = 2 * R * M * N + 2 * R * N
BYTES = R * S * 4 + R * N * 4 + R * M * 2 + R * (N // OFFSETS_IN_A_COLUMN) * 2 + M * N * 4


def tile_lookup_gate_relu_none_kernel(tc, tab, y, w, offs, out):
    nc = tc.nc
    with (
        tc.tile_pool(name="held", bufs=1) as held,
        tc.psum_pool(name="psum", bufs=1) as psum,
    ):
        offsets = held.tile([R, N // OFFSETS_IN_A_COLUMN], U16)
        table = held.tile([R, S], F32)
        stream = held.tile([R, N], F32)
        weights = held.tile([R, M], BF16)
        nc.sync.dma_start(offsets[:], offs)
        nc.scalar.dma_start(table[:], tab)
        nc.sync.dma_start(stream[:], y)
        nc.sync.dma_start(weights[:], w)

        zeros = held.tile([R, 1], F32)
        nc.vector.memset(zeros[:], 0.0)
        warm = held.tile([R, 1], F32)
        nc.scalar.activation(warm[:], zeros[:], RELU)

        gate = held.tile([R, N], F32)
        nc.scalar.activation(gate[:], table[:].indirect(offsets[:]), RELU)

        x = held.tile([R, N], BF16)
        nc.vector.tensor_tensor(x[:], gate[:], stream[:], MULT)

        product = psum.tile([M, N], F32)
        nc.tensor.matmul(product[:], weights[:], x[:], start=True, stop=True)

        result = held.tile([M, N], F32)
        nc.scalar.copy(result[:], product[:])
        nc.scalar.dma_start(out, result[:])
